import numpy as np, ml_dtypes
CORES = [36,164,52,180,100,228,116,244]
N = 8
import mx_ref
BF = ml_dtypes.bfloat16
def gentries(a):
    return np.ascontiguousarray(a.reshape(8, 16, -1).transpose(0, 2, 1)).reshape(8, -1)
def gtable(e):
    e = np.asarray(e); return np.ascontiguousarray(e.reshape(8, -1, 16).transpose(0, 2, 1)).reshape(128, -1).astype(np.int32)
def gcols(t, e):
    v = np.concatenate([t.reshape(8, 16, -1, 4), np.zeros((8, 16, 1, 4), BF)], axis=2)
    return np.ascontiguousarray(np.stack([v[g][:, e[g]] for g in range(8)])).reshape(128, -1)
def tile(rs):
    return np.stack(rs, axis=2).reshape(128, -1).astype(BF)
def pick(q, e):
    c = np.concatenate([q[0].reshape(128, -1, 4), np.zeros((128, 1, 4), np.uint8)], axis=1); s = np.concatenate([q[1], np.ones((16, 1), np.uint8)], axis=1)
    return (np.ascontiguousarray(c[:, e].reshape(128, -1)), np.ascontiguousarray(s[:, e]))
def join(*qs):
    return (np.concatenate([q[0] for q in qs], axis=1), np.concatenate([q[1] for q in qs], axis=1))
def put(q, e, v):
    c, s = q[0].reshape(128, -1, 4).copy(), q[1].copy(); c[:, e] = v[0].reshape(128, -1, 4); s[:, e] = v[1]
    return (c.reshape(128, -1), s)
def pk(c, s):
    return (np.ascontiguousarray(c), mx_ref.live(s))
def emit(q):
    return q[0], q[1]
def packed(v, rng):
    q = [mx_ref.quantize(np.ascontiguousarray(v[r])) for r in range(N)]
    return np.stack([a for a, b in q]), np.stack([mx_ref.plane(b, rng) for a, b in q])
def values_of_codes():
    e, c = np.zeros((128, 128, 4), np.float32), np.zeros((128, 2, 4), np.uint8)
    e[np.arange(128), np.arange(128), 0] = 1
    c[:127, :, 0] = np.arange(256).reshape(2, 128).T[:127]
    return mx_ref.matmul(mx_ref.quantize(e.reshape(128, 512).astype(BF)), (c.reshape(128, 8), np.full((16, 2), 127, np.uint8))).T.reshape(-1).astype(np.float64)
CODE_VALUE, SCALE_VALUE = values_of_codes(), 2.0 ** (np.arange(256) - 127.0)
def decode(q):
    return (CODE_VALUE[q[0]].reshape(16, 8, -1, 4) * SCALE_VALUE[q[1]][:, None, :, None] + 0.0).reshape(128, -1).astype(np.float32)
def f(rng, *shape):
    return mx_ref.flush((rng.standard_normal(shape, dtype=np.float32) * np.exp2(rng.integers(-2, 3, shape[:-1] + (1,)))).astype(BF))
def wide(rng, *shape, cols=0):
    v = rng.standard_normal(shape, dtype=np.float32) * np.exp2(rng.integers(-12, 13, shape)).astype(np.float32)
    if cols: v *= np.repeat(np.exp2(rng.integers(-cols, cols + 1, shape[:-2] + (1, shape[-1] // 4))) * (rng.random(shape[:-2] + (1, shape[-1] // 4)) > 0.0625), 4, axis=-1).astype(np.float32)
    return mx_ref.flush(v.astype(BF))
C = 352
STEP = [4, 1, 2]
def numbers_of(rng):
    return {"x": np.array(f(rng, N, 128, 4 * C)), "u": np.array(f(rng, N, 128, 512)), "v": np.array(f(rng, N, 128, 512))}
def stored(h, t):
    return {"hl": np.stack([gtable(h[r]) for r in range(N)]), "tl": np.stack([gtable(t[r]) for r in range(N)])}
def lists(rng):
    e = np.tile(np.arange(C), (N, 8, 1))
    return stored(rng.permuted(e, axis=2), rng.permuted(e, axis=2))
def layers(rng, still=()):
    w = np.array(f(rng, N, 128, 2048)).reshape(N, 8, 16, 4, 8, 16, 4)
    for i in still:
        w[:, :, i] = 0
        w[:, :, :, :, :, i] = 0
    return w
def weights(rng, w):
    c, s = packed(np.ascontiguousarray(w).reshape(N, 128, 2048), rng)
    return {"wc": c, "ws": s}
def setup_inputs(rng):
    return {**numbers_of(rng), **lists(rng), **weights(rng, layers(rng))}
def setup_inputs_ties(rng):
    d = numbers_of(rng)
    o = rng.permutation(N)
    k = rng.integers(0, 4, (N, 2, 8, C))
    k[o[1]] += 1
    for g in rng.permutation(8)[:4]: k[o[2], :, g] = 1
    x = d["x"].reshape(N, 8, 16, C, 4)
    u = d["u"].reshape(N, 128, 128, 4)
    for i in range(2):
        x[:, :, i] = 0
        x[:, :, i, :, 0] = k[:, i].astype(np.float32).astype(BF)
        u[:, :, i::16] = 0
        for r in range(N):
            for h in range(i, 128, 16): u[r, h, h, 0] = 0.0 if r == o[0] else -1.0 if r == o[1] else 1.0
    a = np.exp2(rng.integers(-3, 4, (8, 1)).astype(np.float32))
    x[:, :, 8:] = 0
    x[:, :, 8, :, 0] = (-1.125 * a).astype(BF)
    x[:, :, 10, :, 0] = (-0.0703125 * a).astype(BF)
    w = layers(rng, [0, 1])
    w[:, :, :, :, :, 8:] = 0
    for g in range(8):
        w[:, g, 8, 0, g, 8, 0] = -28.0
        for b in range(4): w[:, g, 10, b, g, 9, 0] = -2.0 ** (b - 5)
    return {"x": x.reshape(N, 128, 4 * C), "u": u.reshape(N, 128, 512), "v": d["v"], **lists(rng), **weights(rng, w)}
def setup_inputs_near(rng):
    d = numbers_of(rng)
    x = d["x"].astype(np.float32).reshape(N, 8, 16, C, 4)
    x[:, :, 0] = 0
    x[:, :, 8:] = 0
    u = d["u"].reshape(N, 128, 128, 4)
    for i in range(2): u[:, :, i::16] = 0
    w = layers(rng, [0, 8, 9, 10, 11, 12, 13, 14, 15])
    o = rng.permutation(N) % 4
    for r in range(N):
        c = rng.choice([-1.0, 1.0], (8, 1))
        k = 1.0 if o[r] == 0 else 2.0 ** -30
        if o[r] < 2:
            x[r, :, 0, :, 0] = c
            x[r, :, 11, :, 0] = 2.0 ** -10
        x[r, :, 13, :, 0] = rng.integers(0, 2, (8, C)) * (2.0 ** -20 if o[r] < 2 else 2.0 ** -30)
        x[r, :, 15, :, 0] = 2.0 ** -20 if o[r] < 2 else 2.0 ** -29
        for g in range(8):
            w[r, g, 13, 0, g, 12, 0] = 2.0 ** -18 if o[r] < 2 else 2.0 ** -8
            if o[r] < 2: w[r, g, 14, 0, g, 12, 0] = 2.0 ** -6
            w[r, g, 15, 0, g, 15, 0] = 2.0 ** -5 if o[r] < 2 else 16.0
        for i in range(2):
            s = rng.integers(0, 16, (8, C))
            digits = ((s[:, :, None] >> np.arange(4)) & 1) * np.exp2(np.arange(4) - 23.0)
            if o[r] < 2: x[r, :, 8 + i] = digits
            elif o[r] == 2: x[r, :, 8 + i] = digits * rng.choice([-1.0, 1.0], (8, C, 1))
            else:
                x[r, :, 8 + 2 * i, :, 0] = np.where(s < 8, 1.25, 0.0) * 2.0 ** -30 * c
                x[r, :, 9 + 2 * i, :, 0] = np.where(s < 8, 0.0, 1.125) * 2.0 ** -30 * c
                for g in rng.permutation(8)[:4]:
                    e = rng.choice([-1.0, 1.0], C) * 2.0 ** -30
                    x[r, g, 8 + 2 * i, :, 0] = 1.25 * e
                    x[r, g, 9 + 2 * i, :, 0] = -1.125 * e
            for p in range(0, 128, 16):
                u[r, p, p + i, 0] = k if o[r] < 2 else 1.0
                u[r, p + 12, p + i, 0] = k
                if o[r] < 2: u[r, p + 11, p + i, 0] = k
                if o[r] < 3: u[r, p + 8 + i, p + i] = k
                else:
                    u[r, p + 8 + 2 * i, p + i, 0] = k
                    u[r, p + 9 + 2 * i, p + i, 0] = 1.125 * k
        at = [0, C - 1, int(rng.integers(C)), int(rng.integers(C))]
        for g, j in zip(rng.permutation(8)[:4], at): x[r, g, 0, j, 0] = 2.0 ** 29 * rng.choice([-1.0, 1.0])
    return {"x": x.reshape(N, 128, 4 * C).astype(BF), "u": u.reshape(N, 128, 512), "v": d["v"], **lists(rng), **weights(rng, w)}
def setup_inputs_odd(rng):
    d = numbers_of(rng)
    x = (1.0 + (2 * rng.integers(0, 64, (N, 16, 8, C, 4)) + 1) * 2.0 ** -7) * np.exp2(-rng.integers(0, 7, (N, 16, 8, C, 4)).astype(np.float64)) * rng.choice([-1.0, 1.0], (N, 16, 8, C, 4))
    x[:, :, 0, :, 0] = 1.96875 * 2.0 ** 8 * rng.choice([-1.0, 1.0], (N, 16, 1))
    u = d["u"].reshape(N, 128, 128, 4)
    for i in range(2):
        x[:, ::2, 1 + i, :, 0] = (8 + rng.integers(0, 2, (N, 8, C))) * 2.0 ** -8
        u[:, :, i::16] = 0
        for h in range(i, 128, 16): u[:, h + 1, h, 0] = 1.0
    return {"x": x.astype(np.float32).reshape(N, 128, 4 * C).astype(BF), "u": u.reshape(N, 128, 512), "v": d["v"], **lists(rng), **weights(rng, layers(rng, [0, 8]))}
def setup_inputs_ends(rng):
    d = numbers_of(rng)
    x = np.zeros((N, 8, 16, C, 4))
    u = d["u"].astype(np.float32).reshape(N, 128, 128, 4)
    v = d["v"].astype(np.float32)
    w = np.zeros((N, 128, 4, 128, 4), np.float32)
    hh, tt = np.zeros((N, 8, C), np.int64), np.zeros((N, 8, C), np.int64)
    o, e = rng.permutation(N) % 4, rng.permutation(N) % 4
    i, a = np.arange(128), np.arange(C)
    for r in range(N):
        low = -(0.8 + 0.08 * rng.random((8, 16, C, 4))) * 2.0 ** 30
        low[:, 15] = -2.0 ** 30
        tiny = -(1.0 + 0.125 * rng.integers(0, 8, (8, 16, C, 4))) * 2.0 ** -30
        if o[r] == 0: x[r] = low
        if o[r] == 1: x[r] = np.where((rng.random(C) < 0.5)[:, None], -low, low)
        if o[r] == 2: x[r] = tiny
        if o[r] == 3: x[r] = d["x"][r].astype(np.float32).reshape(8, 16, C, 4)[:, :, :1]
        x[r, 0] = tiny[0] * 2.0 ** 20 if o[r] < 2 else tiny[0] if o[r] == 2 else -2.0 ** -30
        for k in range(2):
            h = rng.permutation(8)
            c = np.where(h < 2, 0.0, h % 2 * 2.0 - 1.0)[None, :, None]
            if o[r] < 2: u[r, :, k::16] = c * (0.9 + 0.1 * rng.random((128, 8, 4))) * 2.0 ** 30
            if o[r] == 2: u[r, :, k::16] = c * (1.0 + 0.125 * rng.integers(0, 8, (128, 8, 4))) * 2.0 ** -30
            if o[r] == 3: u[r, :, k::16] *= np.abs(c).astype(np.float32)
        if o[r] < 2: v[r] = rng.choice([-1.0, 1.0], (128, 512)) * (0.9 + 0.1 * rng.random((128, 512))) * 2.0 ** 30
        else: v[r] = rng.choice([-1.0, 1.0], (128, 512)) * (1.0 + 0.125 * rng.integers(0, 8, (128, 512))) * 2.0 ** -30
        k = np.array([0.25, 0.5, 1.0])[rng.permutation(8) % 3] * rng.choice([-1.0, 1.0], 8)
        if o[r] == 2: k[:] = 0.0
        k[0] = 2.0 ** 8 if o[r] > 1 else 2.0 ** -8
        for b in range(4): w[r, i, b, i, b] = np.where((i >= 16) & (i % 16 == 15), 0.0, k[i // 16])
        hh[r] = C - 1 - a if e[r] == 1 else a
        if e[r] == 3: hh[r] = rng.permuted(np.tile(a, (8, 1)), axis=1)
        tt[r] = hh[r] if e[r] < 2 else np.roll(a, 1) if e[r] == 2 else hh[r] ^ 1
    return {"x": x.astype(np.float32).reshape(N, 128, 4 * C).astype(BF), "u": u.reshape(N, 128, 512).astype(BF), "v": v.astype(BF), **stored(hh, tt), **weights(rng, w.astype(BF))}
def setup_inputs_spread(rng):
    d = setup_inputs(rng)
    d["x"] = wide(rng, N, 128, 4 * C, cols=6)
    return d
def check_inputs(d):
    b = []
    for k in ("x", "u", "v"):
        a = np.abs(d[k].astype(np.float32))
        if not (np.isfinite(a).all() and ((a == 0) | (a >= 2.0 ** -30) & (a <= 2.0 ** 30)).all()): b.append("a value of " + k)
    for k in ("hl", "tl"):
        for r in range(N):
            if not (np.sort(gentries(d[k][r]), axis=1) == np.arange(C)).all(): b.append(k + ": every number once in a group")
    none, least, most = [emit(mx_ref.quantize(np.full((128, 16), k, np.float32).astype(BF)))[1][0, 0] for k in (0.0, 2.0 ** -8, 2.0 ** 8)]
    for r in range(N):
        if ((d["wc"][r] == 0x7F) | (d["wc"][r] == 0xFF)).any(): b.append("wc: a code that is no number")
        s = mx_ref.live(d["ws"][r])
        if ((s != none) & ((s < least) | (s > most))).any(): b.append("ws: a scale out of range")
    return b
def ordered(s, a):
    e = np.sort(np.argsort(a, axis=1).reshape(8, -1, 2), axis=2)
    k = np.take_along_axis(s, e.reshape(8, -1), axis=1).reshape(e.shape)
    return np.where((k[:, :, 1] > k[:, :, 0])[:, :, None], e[:, :, ::-1], e).reshape(8, -1)
def transition(s, h, t):
    m = np.zeros((8, C), np.int64)
    np.put_along_axis(m, ordered(s, h), ordered(s, t), axis=1)
    return m
def behind(a, e):
    return np.take_along_axis(a, e, axis=1)
def reference(x, u, v, hl, tl, wc, ws):
    qu = [mx_ref.quantize(u[r]) for r in range(N)]
    lay = [pk(wc[r], ws[r]) for r in range(N)]
    now = [x[r] for r in range(N)]
    head, tail = [gentries(hl[r]) for r in range(N)], [gentries(tl[r]) for r in range(N)]
    for step in STEP:
        way, made = [], []
        for r in range(N):
            s = mx_ref.matmul(qu[r], mx_ref.quantize(now[r])) + np.float32(0.0)
            m0, m1 = transition(s[0::16], head[r], tail[r]), transition(s[1::16], head[r], tail[r])
            way.append(behind(m1, m0))
            z = mx_ref.quantize(((gcols(now[r], m0).astype(np.float32) + gcols(now[r], way[r]).astype(np.float32)) * np.float32(0.5)).astype(BF))
            made.append(mx_ref.quantize(tile([mx_ref.matmul(pick(lay[r], np.arange(128 * b, 128 * b + 128)), z) * np.float32(0.03125) for b in range(4)])))
        for r in range(N):
            p = r ^ step
            far = gcols(decode(made[p]).astype(BF), behind(way[r], way[p]))
            now[r] = (now[r].astype(np.float32) + far.astype(np.float32)).astype(BF)
            head[r], tail[r] = tail[r], behind(head[r], way[p])
    y, tp = np.zeros((N, 128, C), np.float32), np.zeros((N, 8, C), np.float32)
    oc, osc = np.zeros((N, 128, 4 * C), np.uint8), np.zeros((N, 16, C), np.uint8)
    for r in range(N):
        q = mx_ref.quantize(now[r])
        y[r] = mx_ref.matmul(mx_ref.quantize(v[r]), q)
        tp[r] = tail[r]
        oc[r], osc[r] = emit(q)
    return {"y": y, "tp": tp, "oc": oc, "osc": osc}

@@ -1,0 +1,471 @@
+from concourse.bass import DstId, RemoteDMATransfer
+from concourse.mybir import dt, AluOpType, ActivationFunctionType
+
+C = 352
+K = 22
+HV = 176
+SL = 192
+ROUNDS = 3
+STEP = (4, 1, 2)
+HALF = ((0, 160), (160, 352))
+
+SCRATCH = {}
+LOC = {}
+
+
+def _buf(name, cols, dtype, where="sbuf"):
+    SCRATCH[name] = (where, [128, cols], dtype)
+    LOC[name] = (name, 0, cols)
+
+
+def _pack(name, dtype, parts):
+    n = 0
+    for part, cols in parts:
+        LOC[part] = (name, n, cols)
+        n += cols
+    SCRATCH[name] = ("sbuf", [128, n], dtype)
+
+
+for _r in range(ROUNDS + 1):
+    _buf("x%d" % _r, 4 * C, "bfloat16")
+    _buf("xq%d" % _r, C, "float8_e4m3fn_x4")
+    _buf("xp%d" % _r, C, "uint8")
+for _r in range(ROUNDS):
+    _buf("xc%d" % _r, 4 * C, "bfloat16")
+    _buf("hq%d" % _r, C, "float8_e4m3fn_x4")
+    _buf("hp%d" % _r, C, "uint8")
+    _buf("lq%d" % _r, C, "float8_e4m3fn_x4")
+    _buf("lp%d" % _r, C, "uint8")
+    _buf("snd%d" % _r, 2 * K, "uint16")
+    _buf("rcv%d" % _r, 2 * K, "uint16")
+for _n, _c, _t in (("zt", 4 * C, "bfloat16"), ("zq", C, "float8_e4m3fn_x4"), ("zp", C, "uint8"), ("ht", 4 * C, "bfloat16"),
+                   ("vp", 4 * C, "bfloat16"), ("dp", 4 * C, "bfloat16"), ("one", 2048, "bfloat16"), ("eb", 2048, "bfloat16"),
+                   ("eq", 512, "float8_e4m3fn_x4"), ("ep", 512, "uint8"), ("ut", 512, "bfloat16"), ("vt", 512, "bfloat16"),
+                   ("uq", 128, "float8_e4m3fn_x4"), ("up", 128, "uint8"), ("uk", 256, "float8_e4m3fn_x4"), ("ukp", 256, "uint8"),
+                   ("vq", 128, "float8_e4m3fn_x4"), ("vpl", 128, "uint8"), ("wq", 512, "float8_e4m3fn_x4"), ("wpl", 512, "uint8"),
+                   ("hlt", 2 * K, "int32"), ("yt", C, "float32"), ("tpf", C, "float32")):
+    _buf(_n, _c, _t)
+_LISTS = range(ROUNDS + 1)
+_pack("fw", "float32", [("raw%d" % _i, C) for _i in _LISTS] + [("hx%d" % _i, C) for _i in _LISTS] + [("nrm", 2 * SL)] +
+      [(_n, C) for _n in ("s1", "s0", "so1", "so0", "m1f", "ff", "ga", "lf", "pa", "sc1", "sc2", "wl", "iof")] +
+      [("af", C), ("bf", C), ("jm", 16), ("wge", 16), ("weq", 16), ("wls", 16), ("wbs", 16), ("icf", 32)])
+_pack("bw16", "bfloat16", [(_n, C) for _n in ("c1", "c0", "g1", "g0", "gn", "bs1", "bs0", "bsn", "wb")] + [(_n, HV) for _n in ("xb1", "xb0", "nb")])
+_pack("iw", "int32", [("ew%d" % _i, K) for _i in _LISTS] + [("nw%d" % _i, 24) for _i in _LISTS] + [("aw%d" % _r, K) for _r in range(ROUNDS)] + [("bw%d" % _r, K) for _r in range(ROUNDS)] +
+      [(_n, K) for _n in ("w1", "w2", "w3", "w4", "rw", "m1w", "m0w", "dw", "ic", "ic2")] + [("hs", 2 * K), ("hb", 2 * K), ("hb2", 2 * K), ("uoi", 16)])
+_pack("uw", "uint16", [("eu%d" % _i, K) for _i in _LISTS] + [("pu%d" % _i, K) for _i in _LISTS] + [("px%d" % _i, K) for _i in _LISTS] + [("vu%d" % _i, K) for _i in _LISTS] +
+      [("nu%d" % _i, 24) for _i in _LISTS] + [("m4", 4 * K), ("lu", K), ("ks", K), ("uo", 16)])
+for _i in range(8):
+    _buf("b%d" % _i, 512, "float32", "psum")
+
+SEMAPHORES = ["qv", "qs", "qt", "qg", "ldh", "ldt", "ldx", "xc0", "xc1", "xc2", "ldu", "ldv", "ldw", "lds", "oy0", "oy1", "otp", "oc", "os0", "os1", "os2", "os3"]
+for _r in range(ROUNDS):
+    for _n in ("rl", "ra", "rb", "ll", "la", "lb"):
+        SEMAPHORES.append("%s%d" % (_n, _r))
+
+
+def rank_program(g, core, T, topo):
+    rank = T.rank_of(core)
+    if rank is None:
+        return
+    queue = {"v": g.vector, "s": g.scalar, "t": g.tensor, "g": g, "y": g.sync}
+    seen = {e: {} for e in queue}
+    cnt = {}
+    acc = {}
+
+    def clash(a, b):
+        return a[0] == b[0] and a[1] < b[2] and b[1] < a[2] and (a[3] is None or b[3] is None or a[3] == b[3])
+
+    def emit(eng, fn, reads, writes, sem=None, inc=1, events=None):
+        need = {}
+        for regs, wr in ((reads, False), (writes, True)):
+            for rg in regs:
+                for a in acc.get(rg[0], []):
+                    if not clash(rg, a[0]):
+                        continue
+                    if not wr and not a[1] and not (rg[4] and a[2] != eng):
+                        continue
+                    if seen[eng].get(a[3], 0) < a[4] and need.get(a[3], (0,))[0] < a[4]:
+                        need[a[3]] = (a[4], a[5])
+        for s in list(need):
+            for o in need:
+                if o != s and need[o][1].get(s, 0) >= need[s][0]:
+                    del need[s]
+                    break
+        for s in need:
+            queue[eng].wait_ge(T.sem[s], need[s][0])
+            for o in need[s][1]:
+                seen[eng][o] = max(seen[eng].get(o, 0), need[s][1][o])
+            seen[eng][s] = need[s][0]
+        ins = fn()
+        clock = dict(seen[eng])
+        if events is None:
+            s = sem or "q" + eng
+            cnt[s] = cnt.get(s, 0) + inc
+            ins.then_inc(T.sem[s], inc)
+            ev = (s, cnt[s])
+        else:
+            for s, n in events:
+                cnt[s] = cnt.get(s, 0) + n
+            ev = (events[0][0], cnt[events[0][0]])
+        for regs, wr in ((reads, False), (writes, True)):
+            for rg in regs:
+                old = acc.get(rg[0], [])
+                if wr:
+                    old = [a for a in old if not (rg[1] <= a[0][1] and a[0][2] <= rg[2] and (rg[3] is None or rg[3] == a[0][3]))]
+                old.append((rg, wr, eng, ev[0], ev[1], clock))
+                acc[rg[0]] = old
+
+    def st(name, a=0, b=None, step=1):
+        buf, off, n = LOC[name]
+        a, b = off + a, off + (n if b is None else b)
+        return (T[buf][:, a:b:step] if step > 1 else T[buf][:, a:b], [(buf, a, b, None, False)])
+
+    f = st
+
+    def il(name, a, b, e):
+        return (T[name][:, 4 * a + e:4 * b:4], [(name, 4 * a, 4 * b, e, False)])
+
+    def bank(i, n):
+        return (T["b%d" % i][:, 0:n], [("b%d" % i, 0, 512, None, True)])
+
+    def ind(win, off):
+        return (win[0].indirect(off[0]), win[1] + off[1])
+
+    def u32(v):
+        return (v[0].bitcast(dt.uint32), v[1])
+
+    def tt(out, a, b, op):
+        emit("v", lambda: g.vector.tensor_tensor(out[0], a[0], b[0], op), a[1] + b[1], out[1])
+
+    def ts(out, a, c1, op0, c2=None, op1=None, col=None):
+        if op1 is None:
+            emit("v", lambda: g.vector.tensor_scalar(out[0], a[0], c1, None, op0), a[1] + (col or []), out[1])
+        else:
+            emit("v", lambda: g.vector.tensor_scalar(out[0], a[0], c1, c2, op0, op1), a[1] + (col or []), out[1])
+
+    def cp(out, a):
+        emit("v", lambda: g.vector.tensor_copy(out[0], a[0]), a[1], out[1])
+
+    def fill(out, c):
+        emit("v", lambda: g.vector.memset(out[0], c), [], out[1])
+
+    def act(out, a, scale=None):
+        if scale is None:
+            emit("s", lambda: g.scalar.activation(out[0], a[0], ActivationFunctionType.Copy), a[1], out[1])
+        else:
+            emit("s", lambda: g.scalar.activation(out[0], a[0], ActivationFunctionType.Copy, scale=scale), a[1], out[1])
+
+    def scan(out, a, w):
+        emit("v", lambda: g.vector.tensor_tensor_scan(out[0], a[0], w[0], 0.0, AluOpType.add, AluOpType.mult), a[1] + w[1], out[1])
+
+    def quant(codes, plane, src):
+        emit("v", lambda: g.vector.quantize_mx(codes[0], plane[0], src[0]), src[1], codes[1] + plane[1])
+
+    def mm(out, w, ws, m, ms):
+        emit("t", lambda: g.tensor.matmul_mx(out[0], w[0], ws[0], m[0], ms[0], True, True), w[1] + ws[1] + m[1] + ms[1], out[1])
+
+    def iota(out, pattern, base, cm, imprecise):
+        if imprecise:
+            emit("g", lambda: g.iota(out[0], pattern, base, cm, allow_small_or_imprecise_dtypes=True), [], out[1])
+        else:
+            emit("g", lambda: g.iota(out[0], pattern, base, cm), [], out[1])
+
+    def load(eng, sem, name, src, a=0, b=None, codes=False):
+        o = st(name, a, b)
+        emit(eng, lambda: queue[eng].dma_start(o[0].bitcast(dt.uint8) if codes else o[0], src[:, :]), [], o[1], sem=sem, inc=16)
+
+    def store(eng, sem, dst, src, regs):
+        emit(eng, lambda: queue[eng].dma_start(dst, src), regs, [], sem=sem, inc=16)
+
+    def wrap(scr, src):
+        scan(f(scr), src, f("wl"))
+
+    def whole(out, scr):
+        ts(out, st(scr, 15, C, 16), 2.0 ** 15, AluOpType.mult, 0.15, AluOpType.add)
+
+    def bits(out, scr):
+        ts(out, st(scr, 15, C, 16), 2.0 ** -11, AluOpType.is_gt)
+
+    add, sub, mult = AluOpType.add, AluOpType.subtract, AluOpType.mult
+
+    load("y", "ldh", "hlt", T.hl, 0, K)
+    load("s", "ldt", "hlt", T.tl, K, 2 * K)
+    load("y", "ldx", "x0", T.x)
+    load("s", "ldu", "ut", T.u)
+    load("y", "ldw", "wq", T.wc, codes=True)
+    load("y", "lds", "wpl", T.ws)
+    load("y", "ldv", "vt", T.v)
+    load("y", "xc0", "xc0", T.x)
+
+    fill(f("one"), 1.0)
+    iota(f("ic"), [[0, K]], 0, 1, False)
+    iota(f("jm"), [[1, 16]], 0, 0, True)
+    iota(f("iof"), [[1, C]], 0, 0, True)
+    iota(f("uoi"), [[1, 2], [16, 8]], 0, 0, False)
+    ts(f("ic2"), f("ic"), 15, AluOpType.bitwise_and)
+    cp(f("icf", 0, K), f("ic2"))
+    cp(f("ks"), f("ic2"))
+    own = f("icf", 0, 1)
+    ts(f("wge"), f("jm"), own[0], AluOpType.is_ge, col=own[1])
+    for tab, big, end, out in (("wls", 2.0 ** 15, 2.0 ** -30, "wl"), ("wbs", 2.0 ** 10, 2.0 ** -20, "wb")):
+        ts(f("weq"), f("jm"), own[0], AluOpType.is_equal, big - 1.0, mult, col=own[1])
+        tt(f(tab), f("weq"), f("wge"), add)
+        ts(f(tab, 15, 16), f(tab, 15, 16), end, mult)
+        act(f(out), ind(f(tab), f("ks")))
+    cp(f("uo"), f("uoi"))
+    for i in range(ROUNDS + 1):
+        fill(f("nw%d" % i), 0)
+    emit("g", lambda: g.affine_select(T.eb[:, :], T.one[:, :], [[1, 4], [-1, 512]], AluOpType.is_equal, 0.0, 0, 4), f("one")[1], f("eb")[1])
+
+    def inverse(i):
+        o, w = ind(f("raw%d" % i), f("eu%d" % i)), f("iof")
+        emit("v", lambda: g.vector.tensor_copy(o[0], w[0]), f("eu%d" % i)[1] + w[1], f("raw%d" % i)[1])
+
+    def ordered(i, scr):
+        wrap(scr, f("raw%d" % i))
+        whole(f("rw"), scr)
+        tt(f("nw%d" % i, 0, 11), f("rw", 0, 11), f("rw", 11, K), AluOpType.min)
+        tt(f("nw%d" % i, 12, 23), f("rw", 0, 11), f("rw", 11, K), AluOpType.max)
+        cp(f("nu%d" % i), f("nw%d" % i))
+
+    def places_a(i):
+        tt(f("nb"), f("raw%d" % i, 0, HV), f("raw%d" % i, HV, C), AluOpType.is_gt)
+        ts(f("w1"), f("ew%d" % i), HV, AluOpType.is_ge)
+        ts(f("w2"), f("w1"), -HV, mult)
+        tt(f("w3"), f("w2"), f("ew%d" % i), add)
+        cp(f("vu%d" % i), f("w3"))
+
+    def places_b(i):
+        act(f("gn"), ind(f("nb"), f("vu%d" % i)))
+
+    def places_c(i):
+        scan(f("bsn"), f("gn"), f("wb"))
+        bits(f("w2"), "bsn")
+        tt(f("w4"), f("w2"), f("w1"), AluOpType.not_equal)
+        ts(f("w2"), f("w4"), SL, mult)
+        tt(f("w1"), f("w2"), f("w3"), add)
+        cp(f("pu%d" % i), f("w1"))
+        ts(f("w2"), f("w4"), -SL, mult, SL, add)
+        tt(f("w4"), f("w2"), f("w3"), add)
+        cp(f("px%d" % i), f("w4"))
+
+    def choices_a(r):
+        act(f("af"), ind(f("nrm"), f("pu%d" % r)))
+        act(f("bf"), ind(f("nrm"), f("px%d" % r)))
+
+    def choices_b(r):
+        wrap("sc1", f("af"))
+        whole(f("aw%d" % r), "sc1")
+
+    def choices_c(r):
+        wrap("sc2", f("bf"))
+        whole(f("w2"), "sc2")
+        tt(f("bw%d" % r), f("w2"), f("aw%d" % r), sub)
+
+    def flat(out, lst):
+        act(f(out), ind(f("iof"), lst))
+
+    ts(f("hb"), f("hlt"), 1, AluOpType.bitwise_and)
+    ts(f("hs"), f("hlt"), 1, AluOpType.arith_shift_right)
+    ts(f("hb2"), f("hb"), HV, mult)
+    for i in range(2):
+        tt(f("ew%d" % i), f("hb2", i * K, i * K + K), f("hs", i * K, i * K + K), add)
+        cp(f("eu%d" % i), f("ew%d" % i))
+        inverse(i)
+    places_a(0)
+    places_b(0)
+    quant(f("uq"), f("up"), f("ut"))
+    for k in (1, 0):
+        cp(u32(f("uk", 128 * k, 128 * k + 128)), ind(u32(f("uq")), f("uo", 8 * k, 8 * k + 8)))
+        act(f("ukp", 128 * k, 128 * k + 128), ind(f("up"), f("uo", 8 * k, 8 * k + 8)))
+    ordered(1, "sc2")
+    flat("nrm", f("nu1"))
+    places_c(0)
+    choices_a(0)
+    ordered(0, "sc1")
+    quant(f("xq0"), f("xp0"), f("x0"))
+
+    def far(name, a, b, sem, n):
+        acc.setdefault(name, []).append(((name, a, b, None, False), True, "far", sem, n, {}))
+
+    def send_lists(r):
+        d = T.cores[rank ^ STEP[r]]
+        rid, pid = topo.addr(d, core)
+        n = len(topo.engines(core, d))
+        emit("g", lambda: g.remote_dma(T["rcv%d" % r][:, :], T["snd%d" % r][:, :], T.sem["rl%d" % r], T.sem["ll%d" % r], pid, rid, topo.mask(core, d)),
+             f("snd%d" % r)[1], [], events=[("ll%d" % r, n)])
+        cnt["rl%d" % r] = n
+        far("rcv%d" % r, 0, 2 * K, "rl%d" % r, n)
+
+    def send_codes(r, h):
+        a, b = HALF[h]
+        d = T.cores[rank ^ STEP[r]]
+        rid, pid = topo.addr(d, core)
+        eng = topo.engines(core, d)
+        if h:
+            eng = eng[2:] + eng[:2]
+        parts = [eng[0:2], eng[2:4], eng[4:6], eng[6:7], eng[7:8]]
+        rs, ls = ("ra", "rb")[h] + str(r), ("la", "lb")[h] + str(r)
+        q = (b - a) // 4
+
+        def call():
+            tr = []
+            for i in range(5):
+                if i < 4:
+                    src = T["hq%d" % r][:, a + i * q:a + i * q + q].bitcast(dt.uint8)
+                    dst = T["lq%d" % r][:, a + i * q:a + i * q + q].bitcast(dt.uint8)
+                else:
+                    src, dst = T["hp%d" % r][:, a:b], T["lp%d" % r][:, a:b]
+                tr.append(RemoteDMATransfer(dst_ids=[DstId(rid=rid, pnc=pid)], dma_engine_mask=sum(1 << e for e in parts[i]),
+                                            remote_sem=T.sem[rs], src=src, dst=dst))
+            return g.remote_dma_fused(tr, local_sem=T.sem[ls])
+        n = sum(len(p) for p in parts)
+        emit("g", call, f("hq%d" % r, a, b)[1] + f("hp%d" % r, a, b)[1], [], events=[(ls, n)])
+        cnt[rs] = n
+        far("lq%d" % r, a, b, rs, n)
+        far("lp%d" % r, a, b, rs, n)
+
+    for r in range(ROUNDS):
+        X, N, last = "x%d" % r, "x%d" % (r + 1), r == ROUNDS - 1
+        xq, xp, hq, hp, lq, lp, snd, rcv = ["%s%d" % (n, r) for n in ("xq", "xp", "hq", "hp", "lq", "lp", "snd", "rcv")]
+        I, O = r, r + 1
+        def copy_x():
+            o = f("xc%d" % r)
+            emit("y", lambda: g.sync.dma_start(o[0], T[X][:, :]), f(X)[1], o[1], sem="xc%d" % r, inc=16)
+        if r:
+            quant(f(xq), f(xp), f(X))
+            copy_x()
+        for k in (1, 0):
+            for s in range(2):
+                mm(bank(2 * (1 - k) + s, HV), f("uk", 128 * k, 128 * k + 128), f("ukp", 128 * k, 128 * k + 128), f(xq, HV * s, HV * s + HV), f(xp, HV * s, HV * s + HV))
+        if not last:
+            places_a(O)
+        act(f("s1", 0, HV), bank(0, HV))
+        cp(f("s1", HV, C), bank(1, HV))
+        cp(f("s0", 0, HV), bank(2, HV))
+        cp(f("s0", HV, C), bank(3, HV))
+        choices_b(r)
+        first = [f("nu%d" % i, 0, 11) for i in (I, O)]
+        other = [f("nu%d" % i, 12, 23) for i in (I, O)]
+        for k in (1, 0):
+            for i in range(2):
+                act(f("so%d" % k, HV * i, HV * i + HV), ind(f("s%d" % k), other[i]))
+
+        def decide(k):
+            for i in range(2):
+                tt(f("c%d" % k, HV * i, HV * i + HV), ind(f("s%d" % k), first[i]), f("so%d" % k, HV * i, HV * i + HV), AluOpType.is_ge)
+            tt(f("xb%d" % k), f("c%d" % k, 0, HV), f("c%d" % k, HV, C), AluOpType.not_equal)
+            act(f("g%d" % k), ind(f("xb%d" % k), f("vu%d" % I)))
+
+        def onward(k):
+            scan(f("bs%d" % k), f("g%d" % k), f("wb"))
+            bits(f("w4"), "bs%d" % k)
+            tt(f("dw"), f("w4"), f("bw%d" % r), mult)
+            tt(f("m%dw" % k), f("dw"), f("aw%d" % r), add)
+
+        def fours(b):
+            ts(f("m4", b * K, b * K + K), f("m1w"), 4, mult, b, add)
+
+        def second(b):
+            tt(f("vp", b * C, b * C + C), ind(f(X), f("m4", b * K, b * K + K)), il("xc%d" % r, 0, C, b), add)
+        decide(1)
+        decide(0)
+        if not last:
+            places_b(O)
+        if r < 2:
+            flat("hx%d" % r, f("eu%d" % r))
+        choices_c(r)
+        onward(1)
+        fours(0)
+        second(0)
+        fours(1)
+        onward(0)
+        cp(f(snd, K, 2 * K), f("m0w"))
+        cp(f(snd, 0, K), f("m1w"))
+        send_lists(r)
+        second(1)
+        fours(2)
+        second(2)
+        fours(3)
+        second(3)
+
+        def zpart(eng, b, h):
+            a, c = HALF[h]
+            src = ind(f("vp", b * C, b * C + C), f(snd, K + a // 16, K + c // 16))
+            if eng == "s":
+                act(il("zt", a, c, b), src, 0.5)
+            else:
+                ts(il("zt", a, c, b), src, 0.5, mult)
+        for h in range(2):
+            for b in range(3):
+                zpart("s", b, h)
+        for h in range(2):
+            a, c = HALF[h]
+            zpart("v", 3, h)
+            quant(f("zq", a, c), f("zp", a, c), f("zt", 4 * a, 4 * c))
+            for b in range(4):
+                mm(bank(4 * h + b, c - a), f("wq", 128 * b, 128 * b + 128), f("wpl", 128 * b, 128 * b + 128), f("zq", a, c), f("zp", a, c))
+
+        def hpart(b, h):
+            a, c = HALF[h]
+            if b % 2 == 0:
+                act(il("ht", a, c, b), bank(4 * h + b, c - a), 0.03125)
+            else:
+                ts(il("ht", a, c, b), bank(4 * h + b, c - a), 0.03125, mult)
+        for h in range(2):
+            a, c = HALF[h]
+            for b in range(4):
+                hpart(b, h)
+            quant(f(hq, a, c), f(hp, a, c), f("ht", 4 * a, 4 * c))
+            send_codes(r, h)
+        if r == 0:
+            quant(f("eq"), f("ep"), f("eb"))
+        f1, f0 = f(rcv, 0, K), f(rcv, K, 2 * K)
+        act(f("pa"), ind(f("hx%d" % r), f1))
+        act(f("hx%d" % (r + 2)) if r < 2 else f("af"), ind(f("pa"), f0))
+        flat("m1f", f(snd, 0, K))
+        act(f("ff"), ind(f("m1f"), f(snd, K, 2 * K)))
+        act(f("ga"), ind(f("ff"), f1))
+        act(f("lf"), ind(f("ga"), f0))
+        if not last:
+            n = r + 2
+            places_c(O)
+            wrap("sc1", f("hx%d" % n))
+            whole(f("eu%d" % n), "sc1")
+            inverse(n)
+            whole(f("ew%d" % n), "sc1")
+            ordered(n, "sc2")
+            wrap("sc2", f("lf"))
+            whole(f("lu"), "sc2")
+        else:
+            wrap("sc2", f("lf"))
+            whole(f("lu"), "sc2")
+            ts(f("pa"), f("af"), HV, AluOpType.is_ge, 2.0 * HV - 1.0, mult)
+            ts(f("ga"), f("af"), 2.0, mult)
+            tt(f("tpf"), f("ga"), f("pa"), sub)
+            store("y", "otp", T.tp[:, :], T.tpf[0:128:16, :], f("tpf")[1])
+            quant(f("vq"), f("vpl"), f("vt"))
+        for h in range(2):
+            a, c = HALF[h]
+            for b in range(4):
+                mm(bank(4 * h + b, c - a), f("eq", 128 * b, 128 * b + 128), f("ep", 128 * b, 128 * b + 128), f(lq, a, c), f(lp, a, c))
+                act(f("dp", b * C + a, b * C + c), bank(4 * h + b, c - a))
+        if not last:
+            flat("nrm", f("nu%d" % n))
+            choices_a(r + 1)
+        for b in range(4):
+            tt(il(N, 0, C, b), ind(f("dp", b * C, b * C + C), f("lu")), il(X, 0, C, b), add)
+    xq, xp = "xq%d" % ROUNDS, "xp%d" % ROUNDS
+    quant(f(xq), f(xp), f("x%d" % ROUNDS))
+    for s in range(2):
+        mm(bank(s, HV), f("vq"), f("vpl"), f(xq, HV * s, HV * s + HV), f(xp, HV * s, HV * s + HV))
+    store("y", "oc", T.oc[:, :], T[xq][:, :].bitcast(dt.uint8), f(xq)[1])
+    for k in range(4):
+        store("y", "os%d" % k, T.osc[4 * k:4 * k + 4, :], T[xp][32 * k:32 * k + 4, :], f(xp)[1])
+    act(f("yt", 0, HV), bank(0, HV))
+    cp(f("yt", HV, C), bank(1, HV))
+    store("s", "oy0", T.y[:, 0:HV], T.yt[:, 0:HV], f("yt", 0, HV)[1])
+    store("y", "oy1", T.y[:, HV:C], T.yt[:, HV:C], f("yt", HV, C)[1])
+    for s in cnt:
+        if seen["y"].get(s, 0) < cnt[s]:
+            g.sync.wait_ge(T.sem[s], cnt[s])

@@ -1,4 +1,3 @@
-from concourse.bass import DstId, RemoteDMATransfer
 from concourse.mybir import dt, AluOpType, ActivationFunctionType
 
 C = 352
@@ -46,20 +45,20 @@ for _n, _c, _t in (("zt", 4 * C, "bfloat16"), ("zq", C, "float8_e4m3fn_x4"), ("z
                    ("hlt", 2 * K, "int32"), ("yt", C, "float32"), ("tpf", C, "float32")):
     _buf(_n, _c, _t)
 _LISTS = range(ROUNDS + 1)
-_pack("fw", "float32", [("raw%d" % _i, C) for _i in _LISTS] + [("hx%d" % _i, C) for _i in _LISTS] + [("nrm", 2 * SL)] +
-      [(_n, C) for _n in ("s1", "s0", "so1", "so0", "m1f", "ff", "ga", "lf", "pa", "sc1", "sc2", "wl", "iof")] +
-      [("af", C), ("bf", C), ("jm", 16), ("wge", 16), ("weq", 16), ("wls", 16), ("wbs", 16), ("icf", 32)])
-_pack("bw16", "bfloat16", [(_n, C) for _n in ("c1", "c0", "g1", "g0", "gn", "bs1", "bs0", "bsn", "wb")] + [(_n, HV) for _n in ("xb1", "xb0", "nb")])
-_pack("iw", "int32", [("ew%d" % _i, K) for _i in _LISTS] + [("nw%d" % _i, 24) for _i in _LISTS] + [("aw%d" % _r, K) for _r in range(ROUNDS)] + [("bw%d" % _r, K) for _r in range(ROUNDS)] +
-      [(_n, K) for _n in ("w1", "w2", "w3", "w4", "rw", "m1w", "m0w", "dw", "ic", "ic2")] + [("hs", 2 * K), ("hb", 2 * K), ("hb2", 2 * K), ("uoi", 16)])
-_pack("uw", "uint16", [("eu%d" % _i, K) for _i in _LISTS] + [("pu%d" % _i, K) for _i in _LISTS] + [("px%d" % _i, K) for _i in _LISTS] + [("vu%d" % _i, K) for _i in _LISTS] +
-      [("nu%d" % _i, 24) for _i in _LISTS] + [("m4", 4 * K), ("lu", K), ("ks", K), ("uo", 16)])
+_pack("fw", "float32", [("raw%d" % _i, C) for _i in _LISTS] + [("hx%d" % _i, C) for _i in _LISTS] + [("nrm", 3 * SL)] +
+      [(_n, C) for _n in ("s1", "s0", "m1f", "ff", "ga", "lf", "pa", "sc1", "sc2", "sc3", "iof", "tpa")] + [("so1", 2 * SL), ("so0", 2 * SL), ("ab", 2 * C), ("scd", 2 * C), ("wl", 2 * C)] +
+      [("jm", 16), ("wge", 16), ("weq", 16), ("wls", 16), ("wbs", 16), ("icf", 32)] +
+      [("%s%d" % (_n, _r), 24) for _n in ("aw", "bw") for _r in _LISTS] + [("lw", 48), ("hw", 48)] + [(_n, 24) for _n in ("m1w", "m0w", "d1w", "d0w")])
+_pack("bw16", "bfloat16", [(_n, C) for _n in ("g1", "g0", "gn", "bs1", "bs0", "bsn", "wb")] + [("c1", 2 * SL), ("c0", 2 * SL)] + [(_n, HV) for _n in ("xb1", "xb0", "nb")])
+_pack("iw", "int32", [(_n, 4 * K) for _n in ("ew", "half", "less", "vert")] + [(_n, K) for _n in ("w4", "w5", "w6", "w7")] + [("ic", 2 * K), ("ic2", 2 * K)] + [("hs", 2 * K), ("hb", 2 * K), ("hb2", 2 * K), ("uoi", 16)])
+_pack("uw", "uint16", [("eu", 4 * K), ("vu", 4 * K)] + [("pu%d" % _i, K) for _i in _LISTS] +
+      [("nlo", 12 * (ROUNDS + 1)), ("nhi", 12 * (ROUNDS + 1)), ("lu", K), ("ks", 2 * K), ("uo", 16)])
 for _i in range(8):
     _buf("b%d" % _i, 512, "float32", "psum")
 
-SEMAPHORES = ["qv", "qs", "qt", "qg", "ldh", "ldt", "ldx", "xc0", "xc1", "xc2", "ldu", "ldv", "ldw", "lds", "oy0", "oy1", "otp", "oc", "os0", "os1", "os2", "os3"]
+SEMAPHORES = ["qv", "qs", "qt", "qg", "ldh", "ldt", "ldx", "ldu", "ldv", "ldw", "lds", "oy0", "oy1", "otp", "oc", "os0", "os1", "os2", "os3"]
 for _r in range(ROUNDS):
-    for _n in ("rl", "ra", "rb", "ll", "la", "lb"):
+    for _n in ("rl", "ra", "rb", "rp", "ll", "la", "lb", "lp"):
         SEMAPHORES.append("%s%d" % (_n, _r))
 
 
@@ -177,14 +176,16 @@ def rank_program(g, core, T, topo):
     def store(eng, sem, dst, src, regs):
         emit(eng, lambda: queue[eng].dma_start(dst, src), regs, [], sem=sem, inc=16)
 
+    LS, BS = 15, 14
+
     def wrap(scr, src):
-        scan(f(scr), src, f("wl"))
+        scan(f(scr), src, f("wl", 0, C))
 
     def whole(out, scr):
-        ts(out, st(scr, 15, C, 16), 2.0 ** 15, AluOpType.mult, 0.15, AluOpType.add)
+        ts(out, st(scr, 15, C, 16), 2.0 ** LS, AluOpType.mult, 0.15, AluOpType.add)
 
     def bits(out, scr):
-        ts(out, st(scr, 15, C, 16), 2.0 ** -11, AluOpType.is_gt)
+        ts(out, st(scr, 15, C, 16), 2.0 ** (-BS - 1), AluOpType.is_gt)
 
     add, sub, mult = AluOpType.add, AluOpType.subtract, AluOpType.mult
 
@@ -195,94 +196,100 @@ def rank_program(g, core, T, topo):
     load("y", "ldw", "wq", T.wc, codes=True)
     load("y", "lds", "wpl", T.ws)
     load("y", "ldv", "vt", T.v)
-    load("y", "xc0", "xc0", T.x)
 
-    fill(f("one"), 1.0)
-    iota(f("ic"), [[0, K]], 0, 1, False)
+    iota(f("ic"), [[0, 2 * K]], 0, 1, False)
     iota(f("jm"), [[1, 16]], 0, 0, True)
     iota(f("iof"), [[1, C]], 0, 0, True)
     iota(f("uoi"), [[1, 2], [16, 8]], 0, 0, False)
+    iota(f("one"), [[0, 2048]], 1, 0, True)
     ts(f("ic2"), f("ic"), 15, AluOpType.bitwise_and)
-    cp(f("icf", 0, K), f("ic2"))
+    cp(f("icf", 0, K), f("ic2", 0, K))
     cp(f("ks"), f("ic2"))
     own = f("icf", 0, 1)
     ts(f("wge"), f("jm"), own[0], AluOpType.is_ge, col=own[1])
-    for tab, big, end, out in (("wls", 2.0 ** 15, 2.0 ** -30, "wl"), ("wbs", 2.0 ** 10, 2.0 ** -20, "wb")):
+    for tab, big, end, out, n in (("wls", 2.0 ** 15, 2.0 ** (-15 - LS), "wl", 2 * K), ("wbs", 2.0 ** 20, 2.0 ** (-20 - BS), "wb", K)):
         ts(f("weq"), f("jm"), own[0], AluOpType.is_equal, big - 1.0, mult, col=own[1])
         tt(f(tab), f("weq"), f("wge"), add)
         ts(f(tab, 15, 16), f(tab, 15, 16), end, mult)
-        act(f(out), ind(f(tab), f("ks")))
+        act(f(out), ind(f(tab), f("ks", 0, n)))
     cp(f("uo"), f("uoi"))
-    for i in range(ROUNDS + 1):
-        fill(f("nw%d" % i), 0)
+    fill(f("lw"), 0.0)
+    fill(f("hw"), 0.0)
+
+    def side_by_side(r):
+        for b in range(4):
+            o, i = f("xc%d" % r, b * C, b * C + C), il("x%d" % r, 0, C, b)
+            emit("g", lambda: g.affine_select(o[0], i[0], [[0, C]], AluOpType.is_gt, 0.0, 1, 0), i[1], o[1])
+    side_by_side(0)
     emit("g", lambda: g.affine_select(T.eb[:, :], T.one[:, :], [[1, 4], [-1, 512]], AluOpType.is_equal, 0.0, 0, 4), f("one")[1], f("eb")[1])
 
     def inverse(i):
-        o, w = ind(f("raw%d" % i), f("eu%d" % i)), f("iof")
-        emit("v", lambda: g.vector.tensor_copy(o[0], w[0]), f("eu%d" % i)[1] + w[1], f("raw%d" % i)[1])
+        o, w = ind(f("raw%d" % i), f("eu", K * i, K * i + K)), f("iof")
+        emit("v", lambda: g.vector.tensor_copy(o[0], w[0]), f("eu", K * i, K * i + K)[1] + w[1], f("raw%d" % i)[1])
 
-    def ordered(i, scr):
-        wrap(scr, f("raw%d" % i))
-        whole(f("rw"), scr)
-        tt(f("nw%d" % i, 0, 11), f("rw", 0, 11), f("rw", 11, K), AluOpType.min)
-        tt(f("nw%d" % i, 12, 23), f("rw", 0, 11), f("rw", 11, K), AluOpType.max)
-        cp(f("nu%d" % i), f("nw%d" % i))
+    def ordered(i, n):
+        rg = ("fw", C * i, C * (i + n))
+        scan(f("scd", 0, n * C), (T.fw[:, rg[1]:rg[2]], [rg + (None, False)]), f("wl", 0, n * C))
+        for out, tmp, op in (("nlo", "lw", AluOpType.min), ("nhi", "hw", AluOpType.max)):
+            for k in range(n):
+                tt(f(tmp, 12 * (i + k), 12 * (i + k) + 11), st("scd", C * k + 15, C * k + HV, 16), st("scd", C * k + HV + 15, C * k + C, 16), op)
+            ts(f(out, 12 * i, 12 * (i + n)), f(tmp, 12 * i, 12 * (i + n)), 2.0 ** LS, AluOpType.mult, 0.15, AluOpType.add)
 
     def places_a(i):
         tt(f("nb"), f("raw%d" % i, 0, HV), f("raw%d" % i, HV, C), AluOpType.is_gt)
-        ts(f("w1"), f("ew%d" % i), HV, AluOpType.is_ge)
-        ts(f("w2"), f("w1"), -HV, mult)
-        tt(f("w3"), f("w2"), f("ew%d" % i), add)
-        cp(f("vu%d" % i), f("w3"))
+
+    def vertices(i, n):
+        a, b = K * i, K * (i + n)
+        ts(f("half", a, b), f("ew", a, b), HV, AluOpType.is_ge)
+        ts(f("less", a, b), f("half", a, b), -HV, mult)
+        tt(f("vert", a, b), f("less", a, b), f("ew", a, b), add)
+        cp(f("vu", a, b), f("vert", a, b))
 
     def places_b(i):
-        act(f("gn"), ind(f("nb"), f("vu%d" % i)))
+        act(f("gn"), ind(f("nb"), f("vu", K * i, K * i + K)))
 
     def places_c(i):
         scan(f("bsn"), f("gn"), f("wb"))
-        bits(f("w2"), "bsn")
-        tt(f("w4"), f("w2"), f("w1"), AluOpType.not_equal)
-        ts(f("w2"), f("w4"), SL, mult)
-        tt(f("w1"), f("w2"), f("w3"), add)
-        cp(f("pu%d" % i), f("w1"))
-        ts(f("w2"), f("w4"), -SL, mult, SL, add)
-        tt(f("w4"), f("w2"), f("w3"), add)
-        cp(f("px%d" % i), f("w4"))
-
-    def choices_a(r):
-        act(f("af"), ind(f("nrm"), f("pu%d" % r)))
-        act(f("bf"), ind(f("nrm"), f("px%d" % r)))
-
-    def choices_b(r):
-        wrap("sc1", f("af"))
-        whole(f("aw%d" % r), "sc1")
-
-    def choices_c(r):
-        wrap("sc2", f("bf"))
-        whole(f("w2"), "sc2")
-        tt(f("bw%d" % r), f("w2"), f("aw%d" % r), sub)
+        bits(f("w4"), "bsn")
+        tt(f("w5"), f("w4"), f("half", K * i, K * i + K), AluOpType.not_equal)
+        ts(f("w6"), f("w5"), SL, mult)
+        tt(f("w7"), f("w6"), f("vert", K * i, K * i + K), add)
+        cp(f("pu%d" % i), f("w7"))
 
     def flat(out, lst):
-        act(f(out), ind(f("iof"), lst))
+        act(out, ind(f("iof"), lst))
+
+    def out_slots(r):
+        for k, n in enumerate(("nlo", "nhi", "nlo")):
+            flat(f("nrm", SL * k, SL * k + SL), f(n, 12 * (r + 1), 12 * (r + 2)))
+
+    def choices_a(r):
+        for k in range(2):
+            act(f("ab", C * k, C * k + C), ind(f("nrm", SL * k, SL * k + 2 * SL), f("pu%d" % r)))
+
+    def choices_b(r):
+        scan(f("scd"), f("ab"), f("wl"))
+        tt(f("bw%d" % r, 0, K), st("scd", C + 15, 2 * C, 16), st("scd", 15, C, 16), sub)
+        ts(f("aw%d" % r, 0, K), st("scd", 15, C, 16), 2.0 ** -BS, mult)
 
     ts(f("hb"), f("hlt"), 1, AluOpType.bitwise_and)
     ts(f("hs"), f("hlt"), 1, AluOpType.arith_shift_right)
     ts(f("hb2"), f("hb"), HV, mult)
-    for i in range(2):
-        tt(f("ew%d" % i), f("hb2", i * K, i * K + K), f("hs", i * K, i * K + K), add)
-        cp(f("eu%d" % i), f("ew%d" % i))
-        inverse(i)
+    tt(f("ew", 0, 2 * K), f("hb2"), f("hs"), add)
+    cp(f("eu", 0, 2 * K), f("ew", 0, 2 * K))
+    inverse(0)
+    inverse(1)
+    vertices(0, 2)
     places_a(0)
     places_b(0)
     quant(f("uq"), f("up"), f("ut"))
     for k in (1, 0):
         cp(u32(f("uk", 128 * k, 128 * k + 128)), ind(u32(f("uq")), f("uo", 8 * k, 8 * k + 8)))
         act(f("ukp", 128 * k, 128 * k + 128), ind(f("up"), f("uo", 8 * k, 8 * k + 8)))
-    ordered(1, "sc2")
-    flat("nrm", f("nu1"))
+    ordered(0, 2)
+    out_slots(0)
     places_c(0)
     choices_a(0)
-    ordered(0, "sc1")
     quant(f("xq0"), f("xp0"), f("x0"))
 
     def far(name, a, b, sem, n):
@@ -297,97 +304,64 @@ def rank_program(g, core, T, topo):
         cnt["rl%d" % r] = n
         far("rcv%d" % r, 0, 2 * K, "rl%d" % r, n)
 
-    def send_codes(r, h):
-        a, b = HALF[h]
+    def send_run(r, kind, a, b, sem):
+        src, dst = "h%s%d" % (kind, r), "l%s%d" % (kind, r)
         d = T.cores[rank ^ STEP[r]]
         rid, pid = topo.addr(d, core)
-        eng = topo.engines(core, d)
-        if h:
-            eng = eng[2:] + eng[:2]
-        parts = [eng[0:2], eng[2:4], eng[4:6], eng[6:7], eng[7:8]]
-        rs, ls = ("ra", "rb")[h] + str(r), ("la", "lb")[h] + str(r)
-        q = (b - a) // 4
-
-        def call():
-            tr = []
-            for i in range(5):
-                if i < 4:
-                    src = T["hq%d" % r][:, a + i * q:a + i * q + q].bitcast(dt.uint8)
-                    dst = T["lq%d" % r][:, a + i * q:a + i * q + q].bitcast(dt.uint8)
-                else:
-                    src, dst = T["hp%d" % r][:, a:b], T["lp%d" % r][:, a:b]
-                tr.append(RemoteDMATransfer(dst_ids=[DstId(rid=rid, pnc=pid)], dma_engine_mask=sum(1 << e for e in parts[i]),
-                                            remote_sem=T.sem[rs], src=src, dst=dst))
-            return g.remote_dma_fused(tr, local_sem=T.sem[ls])
-        n = sum(len(p) for p in parts)
-        emit("g", call, f("hq%d" % r, a, b)[1] + f("hp%d" % r, a, b)[1], [], events=[(ls, n)])
+        n = len(topo.engines(core, d))
+        rs, ls = "r%s%d" % (sem, r), "l%s%d" % (sem, r)
+        view = (lambda v: v.bitcast(dt.uint8)) if kind == "q" else (lambda v: v)
+        emit("g", lambda: g.remote_dma(view(T[dst][:, a:b]), view(T[src][:, a:b]), T.sem[rs], T.sem[ls], pid, rid, topo.mask(core, d)),
+             f(src, a, b)[1], [], events=[(ls, n)])
         cnt[rs] = n
-        far("lq%d" % r, a, b, rs, n)
-        far("lp%d" % r, a, b, rs, n)
+        far(dst, a, b, rs, n)
 
     for r in range(ROUNDS):
         X, N, last = "x%d" % r, "x%d" % (r + 1), r == ROUNDS - 1
         xq, xp, hq, hp, lq, lp, snd, rcv = ["%s%d" % (n, r) for n in ("xq", "xp", "hq", "hp", "lq", "lp", "snd", "rcv")]
         I, O = r, r + 1
-        def copy_x():
-            o = f("xc%d" % r)
-            emit("y", lambda: g.sync.dma_start(o[0], T[X][:, :]), f(X)[1], o[1], sem="xc%d" % r, inc=16)
         if r:
             quant(f(xq), f(xp), f(X))
-            copy_x()
-        for k in (1, 0):
-            for s in range(2):
-                mm(bank(2 * (1 - k) + s, HV), f("uk", 128 * k, 128 * k + 128), f("ukp", 128 * k, 128 * k + 128), f(xq, HV * s, HV * s + HV), f(xp, HV * s, HV * s + HV))
+            side_by_side(r)
+        for s in range(2):
+            mm(bank(s, HV), f("uk", 128, 256), f("ukp", 128, 256), f(xq, HV * s, HV * s + HV), f(xp, HV * s, HV * s + HV))
+        mm(bank(2, C), f("uk", 0, 128), f("ukp", 0, 128), f(xq), f(xp))
         if not last:
             places_a(O)
         act(f("s1", 0, HV), bank(0, HV))
-        cp(f("s1", HV, C), bank(1, HV))
-        cp(f("s0", 0, HV), bank(2, HV))
-        cp(f("s0", HV, C), bank(3, HV))
-        choices_b(r)
-        first = [f("nu%d" % i, 0, 11) for i in (I, O)]
-        other = [f("nu%d" % i, 12, 23) for i in (I, O)]
+        act(f("s1", HV, C), bank(1, HV))
         for k in (1, 0):
-            for i in range(2):
-                act(f("so%d" % k, HV * i, HV * i + HV), ind(f("s%d" % k), other[i]))
+            if not k:
+                act(f("s0"), bank(2, C))
+            act(f("so%d" % k), ind(f("s%d" % k), f("nhi", 12 * r, 12 * r + 24)))
 
         def decide(k):
-            for i in range(2):
-                tt(f("c%d" % k, HV * i, HV * i + HV), ind(f("s%d" % k), first[i]), f("so%d" % k, HV * i, HV * i + HV), AluOpType.is_ge)
-            tt(f("xb%d" % k), f("c%d" % k, 0, HV), f("c%d" % k, HV, C), AluOpType.not_equal)
-            act(f("g%d" % k), ind(f("xb%d" % k), f("vu%d" % I)))
+            tt(f("c%d" % k), ind(f("s%d" % k), f("nlo", 12 * r, 12 * r + 24)), f("so%d" % k), AluOpType.is_ge)
+            tt(f("xb%d" % k), f("c%d" % k, 0, HV), f("c%d" % k, SL, SL + HV), AluOpType.not_equal)
+            act(f("g%d" % k), ind(f("xb%d" % k), f("vu", K * I, K * I + K)))
 
         def onward(k):
             scan(f("bs%d" % k), f("g%d" % k), f("wb"))
-            bits(f("w4"), "bs%d" % k)
-            tt(f("dw"), f("w4"), f("bw%d" % r), mult)
-            tt(f("m%dw" % k), f("dw"), f("aw%d" % r), add)
-
-        def fours(b):
-            ts(f("m4", b * K, b * K + K), f("m1w"), 4, mult, b, add)
+            tt(f("d%dw" % k, 0, K), st("bs%d" % k, 15, C, 16), f("bw%d" % r, 0, K), mult)
+            tt(f("m%dw" % k, 0, K), f("d%dw" % k, 0, K), f("aw%d" % r, 0, K), add)
+            a = K * (1 - k)
+            ts(f(snd, a, a + K), f("m%dw" % k, 0, K), 2.0 ** (LS + BS), mult, 0.1, add)
 
         def second(b):
-            tt(f("vp", b * C, b * C + C), ind(f(X), f("m4", b * K, b * K + K)), il("xc%d" % r, 0, C, b), add)
+            tt(f("vp", b * C, b * C + C), ind(f("xc%d" % r, b * C, b * C + C), f(snd, 0, K)), il(X, 0, C, b), add)
+        choices_b(r)
         decide(1)
         decide(0)
         if not last:
             places_b(O)
         if r < 2:
-            flat("hx%d" % r, f("eu%d" % r))
-        choices_c(r)
+            flat(f("hx%d" % r), f("eu", K * r, K * r + K))
         onward(1)
-        fours(0)
         second(0)
-        fours(1)
         onward(0)
-        cp(f(snd, K, 2 * K), f("m0w"))
-        cp(f(snd, 0, K), f("m1w"))
         send_lists(r)
-        second(1)
-        fours(2)
-        second(2)
-        fours(3)
-        second(3)
+        for b in range(1, 4):
+            second(b)
 
         def zpart(eng, b, h):
             a, c = HALF[h]
@@ -396,10 +370,10 @@ def rank_program(g, core, T, topo):
                 act(il("zt", a, c, b), src, 0.5)
             else:
                 ts(il("zt", a, c, b), src, 0.5, mult)
-        for h in range(2):
+        for h in range(len(HALF)):
             for b in range(3):
                 zpart("s", b, h)
-        for h in range(2):
+        for h in range(len(HALF)):
             a, c = HALF[h]
             zpart("v", 3, h)
             quant(f("zq", a, c), f("zp", a, c), f("zt", 4 * a, 4 * c))
@@ -408,50 +382,54 @@ def rank_program(g, core, T, topo):
 
         def hpart(b, h):
             a, c = HALF[h]
-            if b % 2 == 0:
+            if b % 2 == 0 or b == 1 and not last:
                 act(il("ht", a, c, b), bank(4 * h + b, c - a), 0.03125)
             else:
                 ts(il("ht", a, c, b), bank(4 * h + b, c - a), 0.03125, mult)
-        for h in range(2):
+        if not last:
+            places_c(O)
+        for h in range(len(HALF)):
             a, c = HALF[h]
             for b in range(4):
                 hpart(b, h)
             quant(f(hq, a, c), f(hp, a, c), f("ht", 4 * a, 4 * c))
-            send_codes(r, h)
+            send_run(r, "q", a, c, "ab"[h])
+        send_run(r, "p", 0, C, "p")
         if r == 0:
             quant(f("eq"), f("ep"), f("eb"))
         f1, f0 = f(rcv, 0, K), f(rcv, K, 2 * K)
         act(f("pa"), ind(f("hx%d" % r), f1))
-        act(f("hx%d" % (r + 2)) if r < 2 else f("af"), ind(f("pa"), f0))
-        flat("m1f", f(snd, 0, K))
+        act(f("hx%d" % (r + 2)) if r < 2 else f("tpa"), ind(f("pa"), f0))
+        flat(f("m1f"), f(snd, 0, K))
         act(f("ff"), ind(f("m1f"), f(snd, K, 2 * K)))
         act(f("ga"), ind(f("ff"), f1))
         act(f("lf"), ind(f("ga"), f0))
         if not last:
             n = r + 2
-            places_c(O)
             wrap("sc1", f("hx%d" % n))
-            whole(f("eu%d" % n), "sc1")
+            whole(f("eu", K * n, K * n + K), "sc1")
             inverse(n)
-            whole(f("ew%d" % n), "sc1")
-            ordered(n, "sc2")
-            wrap("sc2", f("lf"))
-            whole(f("lu"), "sc2")
+            ordered(n, 1)
+            if n < ROUNDS:
+                whole(f("ew", K * n, K * n + K), "sc1")
+                vertices(n, 1)
+            out_slots(r + 1)
+            wrap("sc3", f("lf"))
+            whole(f("lu"), "sc3")
         else:
-            wrap("sc2", f("lf"))
-            whole(f("lu"), "sc2")
-            ts(f("pa"), f("af"), HV, AluOpType.is_ge, 2.0 * HV - 1.0, mult)
-            ts(f("ga"), f("af"), 2.0, mult)
+            wrap("sc3", f("lf"))
+            whole(f("lu"), "sc3")
+            ts(f("pa"), f("tpa"), HV, AluOpType.is_ge, 2.0 * HV - 1.0, mult)
+            ts(f("ga"), f("tpa"), 2.0, mult)
             tt(f("tpf"), f("ga"), f("pa"), sub)
             store("y", "otp", T.tp[:, :], T.tpf[0:128:16, :], f("tpf")[1])
             quant(f("vq"), f("vpl"), f("vt"))
-        for h in range(2):
-            a, c = HALF[h]
-            for b in range(4):
+        for b in range(4):
+            for h in range(len(HALF)):
+                a, c = HALF[h]
                 mm(bank(4 * h + b, c - a), f("eq", 128 * b, 128 * b + 128), f("ep", 128 * b, 128 * b + 128), f(lq, a, c), f(lp, a, c))
-                act(f("dp", b * C + a, b * C + c), bank(4 * h + b, c - a))
+                (cp if b == 0 and h else act)(f("dp", b * C + a, b * C + c), bank(4 * h + b, c - a))
         if not last:
-            flat("nrm", f("nu%d" % n))
             choices_a(r + 1)
         for b in range(4):
             tt(il(N, 0, C, b), ind(f("dp", b * C, b * C + C), f("lu")), il(X, 0, C, b), add)

from concourse.mybir import dt, AluOpType, ActivationFunctionType

C = 352
K = 22
HV = 176
SL = 192
ROUNDS = 3
STEP = (4, 1, 2)
HALF = ((0, 160), (160, 352))

SCRATCH = {}
LOC = {}


def _buf(name, cols, dtype, where="sbuf"):
    SCRATCH[name] = (where, [128, cols], dtype)
    LOC[name] = (name, 0, cols)


def _pack(name, dtype, parts):
    n = 0
    for part, cols in parts:
        LOC[part] = (name, n, cols)
        n += cols
    SCRATCH[name] = ("sbuf", [128, n], dtype)


for _r in range(ROUNDS + 1):
    _buf("x%d" % _r, 4 * C, "bfloat16")
    _buf("xq%d" % _r, C, "float8_e4m3fn_x4")
    _buf("xp%d" % _r, C, "uint8")
for _r in range(ROUNDS):
    _buf("xc%d" % _r, 4 * C, "bfloat16")
    _buf("hq%d" % _r, C, "float8_e4m3fn_x4")
    _buf("hp%d" % _r, C, "uint8")
    _buf("lq%d" % _r, C, "float8_e4m3fn_x4")
    _buf("lp%d" % _r, C, "uint8")
    _buf("snd%d" % _r, 2 * K, "uint16")
    _buf("rcv%d" % _r, 2 * K, "uint16")
for _n, _c, _t in (("zt", 4 * C, "bfloat16"), ("zq", C, "float8_e4m3fn_x4"), ("zp", C, "uint8"), ("ht", 4 * C, "bfloat16"),
                   ("vp", 4 * C, "bfloat16"), ("dp", 4 * C, "bfloat16"), ("one", 2048, "bfloat16"), ("eb", 2048, "bfloat16"),
                   ("eq", 512, "float8_e4m3fn_x4"), ("ep", 512, "uint8"), ("ut", 512, "bfloat16"), ("vt", 512, "bfloat16"),
                   ("uq", 128, "float8_e4m3fn_x4"), ("up", 128, "uint8"), ("uk", 256, "float8_e4m3fn_x4"), ("ukp", 256, "uint8"),
                   ("vq", 128, "float8_e4m3fn_x4"), ("vpl", 128, "uint8"), ("wq", 512, "float8_e4m3fn_x4"), ("wpl", 512, "uint8"),
                   ("hlt", 2 * K, "int32"), ("yt", C, "float32"), ("tpf", C, "float32")):
    _buf(_n, _c, _t)
_LISTS = range(ROUNDS + 1)
_pack("fw", "float32", [("raw%d" % _i, C) for _i in _LISTS] + [("hx%d" % _i, C) for _i in _LISTS] + [("nrm", 3 * SL)] +
      [(_n, C) for _n in ("s1", "s0", "m1f", "ff", "ga", "lf", "pa", "sc1", "sc2", "sc3", "iof", "tpa")] + [("so1", 2 * SL), ("so0", 2 * SL), ("ab", 2 * C), ("scd", 2 * C), ("wl", 2 * C)] +
      [("jm", 16), ("wge", 16), ("weq", 16), ("wls", 16), ("wbs", 16), ("icf", 32)] +
      [("%s%d" % (_n, _r), 24) for _n in ("aw", "bw") for _r in _LISTS] + [("lw", 48), ("hw", 48)] + [(_n, 24) for _n in ("m1w", "m0w", "d1w", "d0w")])
_pack("bw16", "bfloat16", [(_n, C) for _n in ("g1", "g0", "gn", "bs1", "bs0", "bsn", "wb")] + [("c1", 2 * SL), ("c0", 2 * SL)] + [(_n, HV) for _n in ("xb1", "xb0", "nb")])
_pack("iw", "int32", [(_n, 4 * K) for _n in ("ew", "half", "less", "vert")] + [(_n, K) for _n in ("w4", "w5", "w6", "w7")] + [("ic", 2 * K), ("ic2", 2 * K)] + [("hs", 2 * K), ("hb", 2 * K), ("hb2", 2 * K), ("uoi", 16)])
_pack("uw", "uint16", [("eu", 4 * K), ("vu", 4 * K)] + [("pu%d" % _i, K) for _i in _LISTS] +
      [("nlo", 12 * (ROUNDS + 1)), ("nhi", 12 * (ROUNDS + 1)), ("lu", K), ("ks", 2 * K), ("uo", 16)])
for _i in range(8):
    _buf("b%d" % _i, 512, "float32", "psum")

SEMAPHORES = ["qv", "qs", "qt", "qg", "ldh", "ldt", "ldx", "ldu", "ldv", "ldw", "lds", "oy0", "oy1", "otp", "oc", "os0", "os1", "os2", "os3"]
for _r in range(ROUNDS):
    for _n in ("rl", "ra", "rb", "rp", "ll", "la", "lb", "lp"):
        SEMAPHORES.append("%s%d" % (_n, _r))


def rank_program(g, core, T, topo):
    rank = T.rank_of(core)
    if rank is None:
        return
    queue = {"v": g.vector, "s": g.scalar, "t": g.tensor, "g": g, "y": g.sync}
    seen = {e: {} for e in queue}
    cnt = {}
    acc = {}

    def clash(a, b):
        return a[0] == b[0] and a[1] < b[2] and b[1] < a[2] and (a[3] is None or b[3] is None or a[3] == b[3])

    def emit(eng, fn, reads, writes, sem=None, inc=1, events=None):
        need = {}
        for regs, wr in ((reads, False), (writes, True)):
            for rg in regs:
                for a in acc.get(rg[0], []):
                    if not clash(rg, a[0]):
                        continue
                    if not wr and not a[1] and not (rg[4] and a[2] != eng):
                        continue
                    if seen[eng].get(a[3], 0) < a[4] and need.get(a[3], (0,))[0] < a[4]:
                        need[a[3]] = (a[4], a[5])
        for s in list(need):
            for o in need:
                if o != s and need[o][1].get(s, 0) >= need[s][0]:
                    del need[s]
                    break
        for s in need:
            queue[eng].wait_ge(T.sem[s], need[s][0])
            for o in need[s][1]:
                seen[eng][o] = max(seen[eng].get(o, 0), need[s][1][o])
            seen[eng][s] = need[s][0]
        ins = fn()
        clock = dict(seen[eng])
        if events is None:
            s = sem or "q" + eng
            cnt[s] = cnt.get(s, 0) + inc
            ins.then_inc(T.sem[s], inc)
            ev = (s, cnt[s])
        else:
            for s, n in events:
                cnt[s] = cnt.get(s, 0) + n
            ev = (events[0][0], cnt[events[0][0]])
        for regs, wr in ((reads, False), (writes, True)):
            for rg in regs:
                old = acc.get(rg[0], [])
                if wr:
                    old = [a for a in old if not (rg[1] <= a[0][1] and a[0][2] <= rg[2] and (rg[3] is None or rg[3] == a[0][3]))]
                old.append((rg, wr, eng, ev[0], ev[1], clock))
                acc[rg[0]] = old

    def st(name, a=0, b=None, step=1):
        buf, off, n = LOC[name]
        a, b = off + a, off + (n if b is None else b)
        return (T[buf][:, a:b:step] if step > 1 else T[buf][:, a:b], [(buf, a, b, None, False)])

    f = st

    def il(name, a, b, e):
        return (T[name][:, 4 * a + e:4 * b:4], [(name, 4 * a, 4 * b, e, False)])

    def bank(i, n):
        return (T["b%d" % i][:, 0:n], [("b%d" % i, 0, 512, None, True)])

    def ind(win, off):
        return (win[0].indirect(off[0]), win[1] + off[1])

    def u32(v):
        return (v[0].bitcast(dt.uint32), v[1])

    def tt(out, a, b, op):
        emit("v", lambda: g.vector.tensor_tensor(out[0], a[0], b[0], op), a[1] + b[1], out[1])

    def ts(out, a, c1, op0, c2=None, op1=None, col=None):
        if op1 is None:
            emit("v", lambda: g.vector.tensor_scalar(out[0], a[0], c1, None, op0), a[1] + (col or []), out[1])
        else:
            emit("v", lambda: g.vector.tensor_scalar(out[0], a[0], c1, c2, op0, op1), a[1] + (col or []), out[1])

    def cp(out, a):
        emit("v", lambda: g.vector.tensor_copy(out[0], a[0]), a[1], out[1])

    def fill(out, c):
        emit("v", lambda: g.vector.memset(out[0], c), [], out[1])

    def act(out, a, scale=None):
        if scale is None:
            emit("s", lambda: g.scalar.activation(out[0], a[0], ActivationFunctionType.Copy), a[1], out[1])
        else:
            emit("s", lambda: g.scalar.activation(out[0], a[0], ActivationFunctionType.Copy, scale=scale), a[1], out[1])

    def scan(out, a, w):
        emit("v", lambda: g.vector.tensor_tensor_scan(out[0], a[0], w[0], 0.0, AluOpType.add, AluOpType.mult), a[1] + w[1], out[1])

    def quant(codes, plane, src):
        emit("v", lambda: g.vector.quantize_mx(codes[0], plane[0], src[0]), src[1], codes[1] + plane[1])

    def mm(out, w, ws, m, ms):
        emit("t", lambda: g.tensor.matmul_mx(out[0], w[0], ws[0], m[0], ms[0], True, True), w[1] + ws[1] + m[1] + ms[1], out[1])

    def iota(out, pattern, base, cm, imprecise):
        if imprecise:
            emit("g", lambda: g.iota(out[0], pattern, base, cm, allow_small_or_imprecise_dtypes=True), [], out[1])
        else:
            emit("g", lambda: g.iota(out[0], pattern, base, cm), [], out[1])

    def load(eng, sem, name, src, a=0, b=None, codes=False):
        o = st(name, a, b)
        emit(eng, lambda: queue[eng].dma_start(o[0].bitcast(dt.uint8) if codes else o[0], src[:, :]), [], o[1], sem=sem, inc=16)

    def store(eng, sem, dst, src, regs):
        emit(eng, lambda: queue[eng].dma_start(dst, src), regs, [], sem=sem, inc=16)

    LS, BS = 15, 14

    def wrap(scr, src):
        scan(f(scr), src, f("wl", 0, C))

    def whole(out, scr):
        ts(out, st(scr, 15, C, 16), 2.0 ** LS, AluOpType.mult, 0.15, AluOpType.add)

    def bits(out, scr):
        ts(out, st(scr, 15, C, 16), 2.0 ** (-BS - 1), AluOpType.is_gt)

    add, sub, mult = AluOpType.add, AluOpType.subtract, AluOpType.mult

    load("y", "ldh", "hlt", T.hl, 0, K)
    load("s", "ldt", "hlt", T.tl, K, 2 * K)
    load("y", "ldx", "x0", T.x)
    load("s", "ldu", "ut", T.u)
    load("y", "ldw", "wq", T.wc, codes=True)
    load("y", "lds", "wpl", T.ws)
    load("y", "ldv", "vt", T.v)

    iota(f("ic"), [[0, 2 * K]], 0, 1, False)
    iota(f("jm"), [[1, 16]], 0, 0, True)
    iota(f("iof"), [[1, C]], 0, 0, True)
    iota(f("uoi"), [[1, 2], [16, 8]], 0, 0, False)
    iota(f("one"), [[0, 2048]], 1, 0, True)
    ts(f("ic2"), f("ic"), 15, AluOpType.bitwise_and)
    cp(f("icf", 0, K), f("ic2", 0, K))
    cp(f("ks"), f("ic2"))
    own = f("icf", 0, 1)
    ts(f("wge"), f("jm"), own[0], AluOpType.is_ge, col=own[1])
    for tab, big, end, out, n in (("wls", 2.0 ** 15, 2.0 ** (-15 - LS), "wl", 2 * K), ("wbs", 2.0 ** 20, 2.0 ** (-20 - BS), "wb", K)):
        ts(f("weq"), f("jm"), own[0], AluOpType.is_equal, big - 1.0, mult, col=own[1])
        tt(f(tab), f("weq"), f("wge"), add)
        ts(f(tab, 15, 16), f(tab, 15, 16), end, mult)
        act(f(out), ind(f(tab), f("ks", 0, n)))
    cp(f("uo"), f("uoi"))
    fill(f("lw"), 0.0)
    fill(f("hw"), 0.0)

    def side_by_side(r):
        for b in range(4):
            o, i = f("xc%d" % r, b * C, b * C + C), il("x%d" % r, 0, C, b)
            emit("g", lambda: g.affine_select(o[0], i[0], [[0, C]], AluOpType.is_gt, 0.0, 1, 0), i[1], o[1])
    side_by_side(0)
    emit("g", lambda: g.affine_select(T.eb[:, :], T.one[:, :], [[1, 4], [-1, 512]], AluOpType.is_equal, 0.0, 0, 4), f("one")[1], f("eb")[1])

    def inverse(i):
        o, w = ind(f("raw%d" % i), f("eu", K * i, K * i + K)), f("iof")
        emit("v", lambda: g.vector.tensor_copy(o[0], w[0]), f("eu", K * i, K * i + K)[1] + w[1], f("raw%d" % i)[1])

    def ordered(i, n):
        rg = ("fw", C * i, C * (i + n))
        scan(f("scd", 0, n * C), (T.fw[:, rg[1]:rg[2]], [rg + (None, False)]), f("wl", 0, n * C))
        for out, tmp, op in (("nlo", "lw", AluOpType.min), ("nhi", "hw", AluOpType.max)):
            for k in range(n):
                tt(f(tmp, 12 * (i + k), 12 * (i + k) + 11), st("scd", C * k + 15, C * k + HV, 16), st("scd", C * k + HV + 15, C * k + C, 16), op)
            ts(f(out, 12 * i, 12 * (i + n)), f(tmp, 12 * i, 12 * (i + n)), 2.0 ** LS, AluOpType.mult, 0.15, AluOpType.add)

    def places_a(i):
        tt(f("nb"), f("raw%d" % i, 0, HV), f("raw%d" % i, HV, C), AluOpType.is_gt)

    def vertices(i, n):
        a, b = K * i, K * (i + n)
        ts(f("half", a, b), f("ew", a, b), HV, AluOpType.is_ge)
        ts(f("less", a, b), f("half", a, b), -HV, mult)
        tt(f("vert", a, b), f("less", a, b), f("ew", a, b), add)
        cp(f("vu", a, b), f("vert", a, b))

    def places_b(i):
        act(f("gn"), ind(f("nb"), f("vu", K * i, K * i + K)))

    def places_c(i):
        scan(f("bsn"), f("gn"), f("wb"))
        bits(f("w4"), "bsn")
        tt(f("w5"), f("w4"), f("half", K * i, K * i + K), AluOpType.not_equal)
        ts(f("w6"), f("w5"), SL, mult)
        tt(f("w7"), f("w6"), f("vert", K * i, K * i + K), add)
        cp(f("pu%d" % i), f("w7"))

    def flat(out, lst):
        act(out, ind(f("iof"), lst))

    def out_slots(r):
        for k, n in enumerate(("nlo", "nhi", "nlo")):
            flat(f("nrm", SL * k, SL * k + SL), f(n, 12 * (r + 1), 12 * (r + 2)))

    def choices_a(r):
        for k in range(2):
            act(f("ab", C * k, C * k + C), ind(f("nrm", SL * k, SL * k + 2 * SL), f("pu%d" % r)))

    def choices_b(r):
        scan(f("scd"), f("ab"), f("wl"))
        tt(f("bw%d" % r, 0, K), st("scd", C + 15, 2 * C, 16), st("scd", 15, C, 16), sub)
        ts(f("aw%d" % r, 0, K), st("scd", 15, C, 16), 2.0 ** -BS, mult)

    ts(f("hb"), f("hlt"), 1, AluOpType.bitwise_and)
    ts(f("hs"), f("hlt"), 1, AluOpType.arith_shift_right)
    ts(f("hb2"), f("hb"), HV, mult)
    tt(f("ew", 0, 2 * K), f("hb2"), f("hs"), add)
    cp(f("eu", 0, 2 * K), f("ew", 0, 2 * K))
    inverse(0)
    inverse(1)
    vertices(0, 2)
    places_a(0)
    places_b(0)
    quant(f("uq"), f("up"), f("ut"))
    for k in (1, 0):
        cp(u32(f("uk", 128 * k, 128 * k + 128)), ind(u32(f("uq")), f("uo", 8 * k, 8 * k + 8)))
        act(f("ukp", 128 * k, 128 * k + 128), ind(f("up"), f("uo", 8 * k, 8 * k + 8)))
    ordered(0, 2)
    out_slots(0)
    places_c(0)
    choices_a(0)
    quant(f("xq0"), f("xp0"), f("x0"))

    def far(name, a, b, sem, n):
        acc.setdefault(name, []).append(((name, a, b, None, False), True, "far", sem, n, {}))

    def send_lists(r):
        d = T.cores[rank ^ STEP[r]]
        rid, pid = topo.addr(d, core)
        n = len(topo.engines(core, d))
        emit("g", lambda: g.remote_dma(T["rcv%d" % r][:, :], T["snd%d" % r][:, :], T.sem["rl%d" % r], T.sem["ll%d" % r], pid, rid, topo.mask(core, d)),
             f("snd%d" % r)[1], [], events=[("ll%d" % r, n)])
        cnt["rl%d" % r] = n
        far("rcv%d" % r, 0, 2 * K, "rl%d" % r, n)

    def send_run(r, kind, a, b, sem):
        src, dst = "h%s%d" % (kind, r), "l%s%d" % (kind, r)
        d = T.cores[rank ^ STEP[r]]
        rid, pid = topo.addr(d, core)
        n = len(topo.engines(core, d))
        rs, ls = "r%s%d" % (sem, r), "l%s%d" % (sem, r)
        view = (lambda v: v.bitcast(dt.uint8)) if kind == "q" else (lambda v: v)
        emit("g", lambda: g.remote_dma(view(T[dst][:, a:b]), view(T[src][:, a:b]), T.sem[rs], T.sem[ls], pid, rid, topo.mask(core, d)),
             f(src, a, b)[1], [], events=[(ls, n)])
        cnt[rs] = n
        far(dst, a, b, rs, n)

    for r in range(ROUNDS):
        X, N, last = "x%d" % r, "x%d" % (r + 1), r == ROUNDS - 1
        xq, xp, hq, hp, lq, lp, snd, rcv = ["%s%d" % (n, r) for n in ("xq", "xp", "hq", "hp", "lq", "lp", "snd", "rcv")]
        I, O = r, r + 1
        if r:
            quant(f(xq), f(xp), f(X))
            side_by_side(r)
        for s in range(2):
            mm(bank(s, HV), f("uk", 128, 256), f("ukp", 128, 256), f(xq, HV * s, HV * s + HV), f(xp, HV * s, HV * s + HV))
        mm(bank(2, C), f("uk", 0, 128), f("ukp", 0, 128), f(xq), f(xp))
        if not last:
            places_a(O)
        act(f("s1", 0, HV), bank(0, HV))
        act(f("s1", HV, C), bank(1, HV))
        for k in (1, 0):
            if not k:
                act(f("s0"), bank(2, C))
            act(f("so%d" % k), ind(f("s%d" % k), f("nhi", 12 * r, 12 * r + 24)))

        def decide(k):
            tt(f("c%d" % k), ind(f("s%d" % k), f("nlo", 12 * r, 12 * r + 24)), f("so%d" % k), AluOpType.is_ge)
            tt(f("xb%d" % k), f("c%d" % k, 0, HV), f("c%d" % k, SL, SL + HV), AluOpType.not_equal)
            act(f("g%d" % k), ind(f("xb%d" % k), f("vu", K * I, K * I + K)))

        def onward(k):
            scan(f("bs%d" % k), f("g%d" % k), f("wb"))
            tt(f("d%dw" % k, 0, K), st("bs%d" % k, 15, C, 16), f("bw%d" % r, 0, K), mult)
            tt(f("m%dw" % k, 0, K), f("d%dw" % k, 0, K), f("aw%d" % r, 0, K), add)
            a = K * (1 - k)
            ts(f(snd, a, a + K), f("m%dw" % k, 0, K), 2.0 ** (LS + BS), mult, 0.1, add)

        def second(b):
            tt(f("vp", b * C, b * C + C), ind(f("xc%d" % r, b * C, b * C + C), f(snd, 0, K)), il(X, 0, C, b), add)
        choices_b(r)
        decide(1)
        decide(0)
        if not last:
            places_b(O)
        if r < 2:
            flat(f("hx%d" % r), f("eu", K * r, K * r + K))
        onward(1)
        second(0)
        onward(0)
        send_lists(r)
        for b in range(1, 4):
            second(b)

        def zpart(eng, b, h):
            a, c = HALF[h]
            src = ind(f("vp", b * C, b * C + C), f(snd, K + a // 16, K + c // 16))
            if eng == "s":
                act(il("zt", a, c, b), src, 0.5)
            else:
                ts(il("zt", a, c, b), src, 0.5, mult)
        for h in range(len(HALF)):
            for b in range(3):
                zpart("s", b, h)
        for h in range(len(HALF)):
            a, c = HALF[h]
            zpart("v", 3, h)
            quant(f("zq", a, c), f("zp", a, c), f("zt", 4 * a, 4 * c))
            for b in range(4):
                mm(bank(4 * h + b, c - a), f("wq", 128 * b, 128 * b + 128), f("wpl", 128 * b, 128 * b + 128), f("zq", a, c), f("zp", a, c))

        def hpart(b, h):
            a, c = HALF[h]
            if b % 2 == 0 or b == 1 and not last:
                act(il("ht", a, c, b), bank(4 * h + b, c - a), 0.03125)
            else:
                ts(il("ht", a, c, b), bank(4 * h + b, c - a), 0.03125, mult)
        if not last:
            places_c(O)
        for h in range(len(HALF)):
            a, c = HALF[h]
            for b in range(4):
                hpart(b, h)
            quant(f(hq, a, c), f(hp, a, c), f("ht", 4 * a, 4 * c))
            send_run(r, "q", a, c, "ab"[h])
        send_run(r, "p", 0, C, "p")
        if r == 0:
            quant(f("eq"), f("ep"), f("eb"))
        f1, f0 = f(rcv, 0, K), f(rcv, K, 2 * K)
        act(f("pa"), ind(f("hx%d" % r), f1))
        act(f("hx%d" % (r + 2)) if r < 2 else f("tpa"), ind(f("pa"), f0))
        flat(f("m1f"), f(snd, 0, K))
        act(f("ff"), ind(f("m1f"), f(snd, K, 2 * K)))
        act(f("ga"), ind(f("ff"), f1))
        act(f("lf"), ind(f("ga"), f0))
        if not last:
            n = r + 2
            wrap("sc1", f("hx%d" % n))
            whole(f("eu", K * n, K * n + K), "sc1")
            inverse(n)
            ordered(n, 1)
            if n < ROUNDS:
                whole(f("ew", K * n, K * n + K), "sc1")
                vertices(n, 1)
            out_slots(r + 1)
            wrap("sc3", f("lf"))
            whole(f("lu"), "sc3")
        else:
            wrap("sc3", f("lf"))
            whole(f("lu"), "sc3")
            ts(f("pa"), f("tpa"), HV, AluOpType.is_ge, 2.0 * HV - 1.0, mult)
            ts(f("ga"), f("tpa"), 2.0, mult)
            tt(f("tpf"), f("ga"), f("pa"), sub)
            store("y", "otp", T.tp[:, :], T.tpf[0:128:16, :], f("tpf")[1])
            quant(f("vq"), f("vpl"), f("vt"))
        for b in range(4):
            for h in range(len(HALF)):
                a, c = HALF[h]
                mm(bank(4 * h + b, c - a), f("eq", 128 * b, 128 * b + 128), f("ep", 128 * b, 128 * b + 128), f(lq, a, c), f(lp, a, c))
                (cp if b == 0 and h else act)(f("dp", b * C + a, b * C + c), bank(4 * h + b, c - a))
        if not last:
            choices_a(r + 1)
        for b in range(4):
            tt(il(N, 0, C, b), ind(f("dp", b * C, b * C + C), f("lu")), il(X, 0, C, b), add)
    xq, xp = "xq%d" % ROUNDS, "xp%d" % ROUNDS
    quant(f(xq), f(xp), f("x%d" % ROUNDS))
    for s in range(2):
        mm(bank(s, HV), f("vq"), f("vpl"), f(xq, HV * s, HV * s + HV), f(xp, HV * s, HV * s + HV))
    store("y", "oc", T.oc[:, :], T[xq][:, :].bitcast(dt.uint8), f(xq)[1])
    for k in range(4):
        store("y", "os%d" % k, T.osc[4 * k:4 * k + 4, :], T[xp][32 * k:32 * k + 4, :], f(xp)[1])
    act(f("yt", 0, HV), bank(0, HV))
    cp(f("yt", HV, C), bank(1, HV))
    store("s", "oy0", T.y[:, 0:HV], T.yt[:, 0:HV], f("yt", 0, HV)[1])
    store("y", "oy1", T.y[:, HV:C], T.yt[:, HV:C], f("yt", HV, C)[1])
    for s in cnt:
        if seen["y"].get(s, 0) < cnt[s]:
            g.sync.wait_ge(T.sem[s], cnt[s])
